import numpy as np
import ml_dtypes


def mxq(x, axis, fmt="e4m3"):
    dtype, down = {"e4m3": (ml_dtypes.float8_e4m3fn, 7), "e5m2": (ml_dtypes.float8_e5m2, 14)}[fmt]
    v = np.moveaxis(np.asarray(x, np.float32).astype(ml_dtypes.bfloat16).astype(np.float64), axis, -1)
    blocks = v.reshape(v.shape[:-1] + (-1, 32))
    amax = np.abs(blocks).max(-1, keepdims=True)
    byte = np.maximum(np.where(amax > 0, np.frexp(amax)[1] - 1 + 127, 0) - down, 1)
    scale = np.exp2(byte - 127.0)
    codes = (blocks / scale).astype(np.float32).astype(dtype).astype(np.float64)
    return np.moveaxis((codes * scale).reshape(v.shape), -1, axis)


WIDE = False


def mx_kscale(k):
    if not WIDE:
        return np.ones(k)
    levels = np.array([10, -10, 5, -5, 0])
    if k % 512:
        return np.exp2(np.random.permutation(np.resize(levels, k // 32))).repeat(32)
    a = np.empty((k // 512, 16))
    for p in range(k // 512):
        a[p, :8] = np.random.permutation(np.resize(levels, 8))
        for g in range(8):
            far = levels[np.abs(levels - a[p, g]) >= 10]
            a[p, g + 8] = far[np.random.randint(len(far))]
    return np.exp2(a.ravel()).repeat(32)


def f64(x):
    return np.asarray(x).astype(np.float64)


def striped(idx):
    return np.tile(idx.reshape(-1, 16).T, (8, 1)).astype(np.uint16)


def unstriped(offs):
    return offs[:16].T.reshape(-1).astype(np.int64)


E2M1 = np.array([0.0, 0.5, 1.0, 1.5, 2.0, 3.0, 4.0, 6.0, -0.0, -0.5, -1.0, -1.5, -2.0, -3.0, -4.0, -6.0])


def pack_weight(w, fmt):
    k, n = w.shape
    w = f64(np.asarray(w, np.float32).astype(ml_dtypes.bfloat16)).reshape(k // 32, 32, n)
    amax = np.abs(w).max(1)
    if fmt == "e4m3":
        byte = np.frexp(amax)[1] - 1 + 127 - 7
    else:
        mant, ex = np.frexp(amax / 6.0)
        byte = np.where(mant > 0.5, ex, ex - 1) + 127
    byte = np.clip(np.where(amax > 0, byte, 1), 1, 254)
    scaled = (w * np.exp2(127.0 - byte)[:, None, :]).reshape(k, n).astype(np.float32)
    by_word = np.ascontiguousarray(scaled.reshape(k // 512, 128, 4, n).transpose(0, 1, 3, 2))
    if fmt == "e4m3":
        words = by_word.astype(ml_dtypes.float8_e4m3fn).view(np.uint8)
    else:
        c = by_word.astype(ml_dtypes.float4_e2m1fn).view(np.uint8) & 0xF
        words = (c[..., 0::2] | (c[..., 1::2] << 4)).reshape(k // 512, 128, 2 * n)
    return np.ascontiguousarray(words), np.ascontiguousarray(byte.astype(np.uint8).reshape(k // 512, 16, n))


def unpack_weight(words, scales, fmt):
    g, _, n = scales.shape
    words = np.ascontiguousarray(words).reshape(g, 128, n, -1)
    if fmt == "e4m3":
        vals = words.view(ml_dtypes.float8_e4m3fn).astype(np.float64)
    else:
        nib = np.empty((g, 128, n, 4), np.uint8)
        nib[..., 0::2] = words & 0xF
        nib[..., 1::2] = words >> 4
        vals = E2M1[nib]
    vals = vals * np.repeat(np.exp2(scales.astype(np.float64) - 127.0), 8, axis=1)[..., None]
    return vals.transpose(0, 1, 3, 2).reshape(g * 512, n)


def gelu(v):
    return 0.5 * v * (1.0 + np.tanh(np.sqrt(2.0 / np.pi) * (v + 0.044715 * v**3)))


def pack_table4(v):
    words, scales = pack_weight(v, "e2m1")
    g, t = words.shape[0] // 2, v.shape[1]
    words = words.reshape(g, 2, 128, t, 2).transpose(0, 2, 3, 1, 4)
    return np.concatenate([words.reshape(g, -1), scales.reshape(g, -1)], axis=1)


def unpack_table4(tab):
    g, t = tab.shape[0], tab.shape[1] // 544
    words = tab[:, :512 * t].reshape(g, 128, t, 2, 2).transpose(0, 3, 1, 2, 4).reshape(2 * g, 128, 2 * t)
    return unpack_weight(words, tab[:, 512 * t:].reshape(2 * g, 16, t), "e2m1")


K, T, S, B, H, N = 1024, 4096, 1536, 512, 1024, 512

def setup_inputs():
    n = np.random.standard_normal
    s = mx_kscale(K)[:, None]
    u = mx_kscale(H)[:, None]
    tab = pack_table4(n((K, T)) * s)
    offs = striped(np.random.permutation(T)[:S])
    ws = (n((K, H)) / np.sqrt(K) / s).astype(np.float32)
    wr_words, wr_scales = pack_weight(n((K, H)) / np.sqrt(K) / s, "e2m1")
    wo = (n((K, H)) / np.sqrt(K) / s).astype(np.float32)
    gain = (np.exp(0.3 * n(H)) * u[:, 0]).astype(np.float32)
    wp_words, wp_scales = pack_weight(n((H, N)) / np.sqrt(H) / u, "e4m3")
    bias = (0.3 * n(N)).astype(np.float32)
    return {"tab": tab, "offs": offs, "ws": ws, "wr_words": wr_words, "wr_scales": wr_scales,
            "wo": wo, "gain": gain, "wp_words": wp_words, "wp_scales": wp_scales, "bias": bias}

def reference(tab, offs, ws, wr_words, wr_scales, wo, gain, wp_words, wp_scales, bias):
    v = unpack_table4(tab)[:, unstriped(offs)]
    wsq = mxq(f64(ws), 0, "e4m3")
    wrq = unpack_weight(wr_words, wr_scales, "e2m1")
    woq = mxq(f64(wo), 0, "e4m3")
    a = wsq.T @ v[:, :B]
    b = wrq.T @ v[:, B:2 * B]
    c = woq.T @ v[:, 2 * B:]
    h = np.tanh(a * b * c) * f64(gain)[:, None]
    hq = mxq(h, 0, "e4m3")
    wpq = unpack_weight(wp_words, wp_scales, "e4m3")
    return (wpq.T @ hq) + f64(bias)[:, None]

from contextlib import ExitStack

import concourse.mybir as mybir

K, T, S, B, H, N = 1024, 4096, 1536, 512, 1024, 512
FLOPS = 2 * (3 * K * H * B + H * N * B)

F32 = mybir.dt.float32
BF16 = mybir.dt.bfloat16
I32 = mybir.dt.int32
U32 = mybir.dt.uint32
U16 = mybir.dt.uint16
U8 = mybir.dt.uint8
FP8X4 = mybir.dt.float8_e4m3fn_x4
FP4X4 = mybir.dt.float4_e2m1fn_x4
MULT = mybir.AluOpType.mult
ADD = mybir.AluOpType.add
COPY = mybir.ActivationFunctionType.Copy
TANH = mybir.ActivationFunctionType.Tanh
IDENTITY = mybir.ActivationFunctionType.Identity

P = 128
PACK = 4
PASS = 512
PASSES = 2
GROUPS = 2
QUARTERS = 4
TOK = 128
SCALE_ROW = 96
SLOT = 4 * PACK * PASS
QUARTER_BYTES = 4 * TOK * PACK


def tile_list_triple_factor_scores_kernel(
    tc, tab, offs, ws, wr_words, wr_scales, wo, gain, wp_words, wp_scales, bias, out
):
    nc = tc.nc
    with ExitStack() as ctx:
        keep = ctx.enter_context(tc.tile_pool(name="keep", bufs=1))
        stage = ctx.enter_context(tc.tile_pool(name="stage", bufs=1))
        ring = ctx.enter_context(tc.tile_pool(name="ring", bufs=4))
        psum = ctx.enter_context(tc.psum_pool(name="psum", bufs=1))

        def staged(shape, dtype, name, slot, begin=0):
            return stage.tile(shape, dtype, name=name, align_bytes=64, offset=slot * SLOT + begin)

        offsets = keep.tile([P, S // 16], U16, name="offsets")
        tab_scales = staged([P, T], U8, "tab_scales", 0)
        tab_words = keep.tile([P, T], I32, name="tab_words", align_bytes=64)
        wr_scale_rows = keep.tile([P, PASSES * H], U8, name="wr_scale_rows", align_bytes=64)
        wr_plane = keep.tile([P, PASSES * H], U8, name="wr_plane", align_bytes=64)
        wr_raw = staged([P, PASSES * 2 * H], U8, "wr_raw", 3, SLOT - 4 * B)
        picked_scales = keep.tile([P, S], U8, name="picked_scales", align_bytes=64)
        v_plane = keep.tile([P, PASSES * S], U8, name="v_plane", align_bytes=64)
        wp_plane = keep.tile([P, PASSES * N], U8, name="wp_plane", align_bytes=64)

        nc.gpsimd.memset(wr_scale_rows[:].bitcast(I32), 0)
        nc.gpsimd.memset(wp_plane[:].bitcast(I32), 0)
        nc.vector.memset(tab_scales[0:SCALE_ROW, :].bitcast(I32), 0)
        nc.vector.memset(v_plane[:].bitcast(I32), 0)

        raw = {}

        def load_weight(name, w, g, a, slot, pieces=1):
            width = PASS // pieces
            raw[name, g, a] = []
            for i in range(pieces):
                piece = staged([P, PACK, width], F32, "raw_%s_%d_%d_%d" % (name, g, a, i), slot, i * SLOT // pieces)
                cols = slice(PASS * g + width * i, PASS * g + width * (i + 1))
                nc.sync.dma_start(
                    out=piece[:], in_=w[PASS * a : PASS * (a + 1), cols].rearrange("(p j) c -> p j c", j=PACK)
                )
                raw[name, g, a].append(piece)

        def load_scale_rows(queue, plane, scales):
            for quad in range(4):
                queue.dma_start(
                    out=plane[32 * quad : 32 * quad + 4, :].bitcast(I32).rearrange("p (a c) -> p a c", a=PASSES),
                    in_=scales[:, 4 * quad : 4 * quad + 4, :].rearrange("a r c -> r a c").bitcast(I32),
                )

        picked = {}
        v_codes = {}

        def gather(role, tile):
            picked[role] = tile
            columns = slice(role * (B // 16), (role + 1) * (B // 16))
            nc.vector.tensor_copy(tile[:], tab_words[:].bitcast(U32).indirect(offsets[:, columns]))

        def part(role):
            v_codes[role] = keep.tile([P, PASSES * 2 * B], U8, name="v_codes_%d" % role, align_bytes=64)
            nc.vector.tensor_copy(
                out=v_codes[role][:].bitcast(U16).rearrange("p (h j) -> p h j", h=PASSES),
                in_=picked[role][:].bitcast(U16).rearrange("p (j h) -> p h j", h=PASSES),
            )

        grouped = {}
        codes = {}
        planes = {}

        def cast_views(key, begin, end):
            if key not in grouped:
                if key == ("ws", 0, 0):
                    grouped[key] = keep.tile([P, PACK * PASS], BF16, name="grouped", tag="first_block", align_bytes=64)
                else:
                    grouped[key] = ring.tile([P, PACK * PASS], BF16, name="grouped", align_bytes=64)
            dst = grouped[key][:].rearrange("p (u e m j) -> p u m j e", u=2, e=2, j=PACK)[:, :, begin:end]
            per_piece = P // len(raw[key])
            piece = raw[key][begin // per_piece]
            src = piece[:].rearrange("p j (m u e) -> p u m j e", u=2, e=2)
            return dst, src[:, :, begin % per_piece : begin % per_piece + end - begin]

        def cast_on_scalar(key, begin=0, end=P):
            dst, src = cast_views(key, begin, end)
            nc.scalar.copy(out=dst, in_=src)

        def cast_on_vector(key, begin=0, end=P):
            dst, src = cast_views(key, begin, end)
            nc.vector.tensor_copy(out=dst, in_=src)

        def quantise(key, tag=None):
            codes[key] = keep.tile([P, PASS], U32, name="codes", tag=tag or "codes_%s_%d_%d" % key, align_bytes=64)
            planes[key] = keep.tile([P, PASS], U8, name="plane_%s_%d_%d" % key, align_bytes=64)
            nc.vector.quantize_mx(out=codes[key][:].bitcast(FP8X4), scales=planes[key][:], in_=grouped[key][:])

        def stationary(name, g, a, t):
            if name == "wr":
                col = a * H + g * PASS + t * P
                return wr_codes[:, 2 * col : 2 * (col + P)].bitcast(FP4X4), wr_plane[:, col : col + P]
            cols = slice(t * P, (t + 1) * P)
            return codes[name, g, a][:, cols].bitcast(FP8X4), planes[name, g, a][:, cols]

        role_of = {"ws": 0, "wr": 1, "wo": 2}
        bank_side = {("wr", 0): 0, ("ws", 0): 1, ("wo", 0): 0, ("wr", 1): 0, ("ws", 1): 1, ("wo", 1): 0}
        banks = {}

        def project(name, g, a, q):
            role = role_of[name]
            if a == 0:
                tag = "bank_%d_%d" % (bank_side[name, g], q)
                banks[name, g, q] = psum.tile([P, PACK, TOK], F32, name="bank", tag=tag)
            col = a * B + q * TOK
            scale_col = a * S + role * B + q * TOK
            for t in range(PACK):
                lhs, lhs_scale = stationary(name, g, a, t)
                nc.tensor.matmul_mx(
                    out=banks[name, g, q][:, t, :],
                    lhsT=lhs,
                    lhsT_scale=lhs_scale,
                    rhs=v_codes[role][:, 2 * col : 2 * (col + TOK)].bitcast(FP4X4),
                    rhs_scale=v_plane[:, scale_col : scale_col + TOK],
                    start=(a == 0 and t == 0),
                    stop=(a == PASSES - 1 and t == PACK - 1),
                )

        def project_pass(name, g, a):
            for q in range(QUARTERS):
                project(name, g, a, q)

        def project_relations(g):
            for q in range(QUARTERS):
                for a in range(PASSES):
                    project("wr", g, a, q)

        def woven(bank):
            return bank[:].rearrange("p t j -> p j t")

        relation = {}
        pair = {}
        triple = {}
        bounded = {}
        scores = {}
        h_codes = {}
        h_planes = {}

        def take_relation(g, q, tile):
            relation[g, q] = tile
            nc.scalar.copy(out=tile[:], in_=woven(banks["wr", g, q]))

        def times_subject(g, q):
            pair[g, q] = keep.tile([P, TOK, PACK], F32, name="pair_%d_%d" % (g, q))
            nc.vector.tensor_tensor(out=pair[g, q][:], in0=woven(banks["ws", g, q]), in1=relation[g, q][:], op=MULT)

        def times_object(g, q):
            triple[g, q] = keep.tile([P, TOK, PACK], F32, name="triple_%d_%d" % (g, q))
            nc.vector.tensor_tensor(out=triple[g, q][:], in0=woven(banks["wo", g, q]), in1=pair[g, q][:], op=MULT)

        def bound(g, q, tile):
            bounded[g, q] = tile
            nc.scalar.activation(out=tile[:], in_=triple[g, q][:], func=TANH)

        def times_gain(g, q, tile):
            scores[g, q] = tile
            nc.vector.tensor_tensor(
                out=tile[:],
                in0=bounded[g, q][:],
                in1=gains[:, g, :].unsqueeze(1).to_broadcast([P, TOK, PACK]),
                op=MULT,
            )

        def quantise_scores(g, q):
            h_codes[g, q] = keep.tile([P, TOK], U32, name="h_codes_%d_%d" % (g, q), align_bytes=64)
            h_planes[g, q] = keep.tile([P, TOK], U8, name="h_plane_%d_%d" % (g, q), align_bytes=64)
            nc.vector.quantize_mx(
                out=h_codes[g, q][:].bitcast(FP8X4),
                scales=h_planes[g, q][:],
                in_=scores[g, q][:].rearrange("p j t -> p (j t)"),
            )

        def read_out(g, q):
            if g == 0:
                banks["out", q] = psum.tile([P, N // P, TOK], F32, name="bank", tag="bank_1_%d" % q)
            for c in range(N // P):
                cols = slice(g * N + c * P, g * N + (c + 1) * P)
                nc.tensor.matmul_mx(
                    out=banks["out", q][:, c, :],
                    lhsT=wp_codes[:, cols].bitcast(FP8X4),
                    lhsT_scale=wp_plane[:, cols],
                    rhs=h_codes[g, q][:].bitcast(FP8X4),
                    rhs_scale=h_planes[g, q][:],
                    start=(g == 0 and c == 0),
                    stop=(g == GROUPS - 1 and c == N // P - 1),
                )

        def store(q):
            result = ring.tile([P, N // P, TOK], F32, name="result")
            if q < QUARTERS - 1:
                for c in range(N // P):
                    nc.scalar.activation(
                        out=result[:, c, :], in_=banks["out", q][:, c, :], func=IDENTITY, bias=biases[:, c : c + 1]
                    )
            else:
                nc.vector.tensor_tensor(
                    out=result[:],
                    in0=banks["out", q][:],
                    in1=biases[:].unsqueeze(2).to_broadcast([P, N // P, TOK]),
                    op=ADD,
                )
            nc.sync.dma_start(out=out.rearrange("(c p) j -> p c j", p=P)[:, :, q * TOK : (q + 1) * TOK], in_=result[:])

        nc.sync.dma_start(offsets[:], offs)
        nc.sync.dma_start(
            out=tab_scales[SCALE_ROW:P, :].bitcast(I32),
            in_=tab[0, PASS * T :].rearrange("(h q t) -> q h t", h=PASSES, t=T).bitcast(I32),
        )
        load_scale_rows(nc.sync, wr_scale_rows, wr_scales)
        for half in range(2):
            cols = slice(half * T // 2, (half + 1) * T // 2)
            nc.sync.dma_start(
                out=tab_words[:, cols], in_=tab[0, 0 : PASS * T].rearrange("(p c) -> p c", p=P).bitcast(I32)[:, cols]
            )
        load_weight("ws", ws, 0, 0, slot=2, pieces=2)
        nc.sync.dma_start(
            out=wr_raw[:].bitcast(I32).rearrange("p (a c) -> p a c", a=PASSES),
            in_=wr_words.rearrange("a p c -> p a c").bitcast(I32),
        )
        load_scale_rows(nc.gpsimd, wp_plane, wp_scales)

        nc.vector.tensor_copy(picked_scales[:], tab_scales[:].indirect(offsets[:]))
        for quad in range(4):
            nc.sync.dma_start(
                out=v_plane[32 * quad : 32 * quad + 4, :].bitcast(I32).rearrange("p (a c) -> p a c", a=PASSES),
                in_=picked_scales[SCALE_ROW + 8 * quad : SCALE_ROW + 8 * quad + 8, :].bitcast(I32),
            )
        load_weight("ws", ws, 0, 1, slot=0)
        nc.vector.tensor_copy(
            out=wr_plane[:].rearrange("p (s t m) -> p s t m", t=PACK, m=P),
            in_=wr_scale_rows[:].rearrange("p (s m t) -> p s t m", t=PACK, m=P),
        )

        gather(0, staged([P, B], U32, "picked_0", 1))
        gather(1, keep.tile([P, B], U32, name="picked_1", align_bytes=64))
        dst, src = cast_views(("ws", 0, 0), 0, P // 2)
        for u in range(2):
            nc.scalar.activation(out=dst[:, u], in_=src[:, u], func=COPY)
        cast_on_scalar(("ws", 0, 0), P // 2, P)
        part(0)
        load_weight("wo", wo, 0, 0, slot=1)
        load_weight("wo", wo, 0, 1, slot=2)
        part(1)
        quantise(("ws", 0, 0))
        project_pass("ws", 0, 0)
        wr_codes = keep.tile([P, PASSES * 2 * H], U8, name="wr_codes", tag="first_block", align_bytes=64)
        nc.vector.tensor_copy(
            out=wr_codes[:].bitcast(U16).rearrange("p (s t m) -> p s t m", t=PACK, m=P),
            in_=wr_raw[:].bitcast(U16).rearrange("p (s m t) -> p s t m", t=PACK, m=P),
        )
        load_weight("ws", ws, 1, 0, slot=3)
        project_relations(0)
        cast_on_scalar(("ws", 0, 1))
        gather(2, staged([P, B], U32, "picked_2", 4))
        quantise(("ws", 0, 1))
        project_pass("ws", 0, 1)
        part(2)
        load_weight("ws", ws, 1, 1, slot=4)
        for q in range(QUARTERS):
            take_relation(0, q, staged([P, TOK, PACK], F32, "relation_0_%d" % q, 0, q * QUARTER_BYTES))
        cast_on_vector(("wo", 0, 0))
        load_weight("wo", wo, 1, 0, slot=1)
        cast_on_scalar(("wo", 0, 1))
        load_weight("wo", wo, 1, 1, slot=2, pieces=2)
        gains = keep.tile([P, GROUPS, PACK], F32, name="gains", tag="picked_scales", align_bytes=64)
        nc.sync.dma_start(out=gains[:], in_=gain.rearrange("(g p t) -> p g t", g=GROUPS, t=PACK))
        wp_codes = keep.tile([P, PASSES * N], I32, name="wp_codes", tag="tab_words", align_bytes=64)
        nc.sync.dma_start(
            out=wp_codes[:].rearrange("p (a c) -> p a c", a=PASSES),
            in_=wp_words.rearrange("a p e i -> p a (e i)").bitcast(I32),
        )
        times_subject(0, 0)
        quantise(("wo", 0, 0))
        project_pass("wo", 0, 0)
        for q in range(1, QUARTERS):
            times_subject(0, q)
        quantise(("wo", 0, 1))
        project_pass("wo", 0, 1)
        biases = keep.tile([P, N // P], F32, name="biases", tag="picked_1", align_bytes=64)
        with nc.allow_non_contiguous_dma(reason="one bias value a partition and output tile"):
            nc.sync.dma_start(out=biases[:], in_=bias.rearrange("(c p) -> p c", p=P))
        cast_on_scalar(("ws", 1, 0))
        cast_on_scalar(("ws", 1, 1))
        for q in range(QUARTERS):
            times_object(0, q)
        project_relations(1)
        quantise(("ws", 1, 0))
        project_pass("ws", 1, 0)
        quantise(("ws", 1, 1))
        project_pass("ws", 1, 1)
        cast_on_scalar(("wo", 1, 0))
        cast_on_vector(("wo", 1, 1), 0, P // 2)
        cast_on_vector(("wo", 1, 1), P // 2, P)
        for q in range(QUARTERS):
            take_relation(1, q, staged([P, TOK, PACK], F32, "relation_1_%d" % q, 1, q * QUARTER_BYTES))
        quantise(("wo", 1, 0))
        quantise(("wo", 1, 1))
        for q in range(QUARTERS):
            for a in range(PASSES):
                project("wo", 1, a, q)
        for step in range(QUARTERS + 1):
            if step < QUARTERS:
                times_subject(1, step)
            if step > 0:
                times_object(1, step - 1)
                bound(0, step - 1, staged([P, TOK, PACK], F32, "bounded_0_%d" % step, 2, (step - 1) * QUARTER_BYTES))
                bound(1, step - 1, ring.tile([P, TOK, PACK], F32, name="bounded"))
        units = [(g, q) for q in range(QUARTERS) for g in range(GROUPS)]
        for step in range(len(units) + 1):
            if step < len(units):
                times_gain(*units[step], ring.tile([P, TOK, PACK], BF16, name="scores", align_bytes=64))
            if step > 0:
                quantise_scores(*units[step - 1])
                read_out(*units[step - 1])
                if units[step - 1][0] == GROUPS - 1:
                    store(units[step - 1][1])
